import numpy as np, ml_dtypes
CORES = [73,201,329,457,330]
N = 5
QP = 128
WID = [128,16,128,16,16]
def setup_inputs(rng):
    return {"q": rng.standard_normal((N, 128, QP), dtype=np.float32).astype(ml_dtypes.bfloat16), "k": rng.standard_normal((N, 128, 128), dtype=np.float32).astype(ml_dtypes.bfloat16), "v": rng.standard_normal((N, 128, 128), dtype=np.float32).astype(ml_dtypes.bfloat16)}
def setup_inputs_big(rng):
    d = setup_inputs(rng)
    for k in ("q", "k", "v"): d[k] = (d[k].astype(np.float32) * 1024.0).astype(d[k].dtype)
    return d
def setup_inputs_small(rng):
    d = setup_inputs(rng)
    for k in ("q", "k", "v"): d[k] = (d[k].astype(np.float32) * (1 / 1024.0)).astype(d[k].dtype)
    return d
def setup_inputs_apart(rng):
    d = setup_inputs(rng)
    f = (10.0 ** rng.permutation(np.linspace(-1.5, 1.5, N))).astype(np.float32).reshape(N, 1, 1)
    for k in ("q", "k", "v"): d[k] = (d[k].astype(np.float32) * f).astype(d[k].dtype)
    return d
def whole(q, k, v):
    Q, K, V = q.astype(np.float64), k.astype(np.float64), v.astype(np.float64)
    y = np.zeros((N, 128, QP))
    for r in range(N):
        S = [K[j].T @ Q[r] for j in range(N)]
        m = np.max([s.max(axis=0) for s in S], axis=0)
        y[r] = sum(V[j].T @ np.maximum(S[j] - 0.5 * m, 0.0) for j in range(N))
    return {"y": y.astype(ml_dtypes.bfloat16)}
def reference(q, k, v):
    o = whole(q, k, v)["y"].copy()
    for r in range(N):
        o[r][:, WID[r]:] = np.nan
    return {"y": o}

@@ -1,0 +1,224 @@
+from concourse.mybir import AluOpType
+
+NB = 5
+BW = 256
+
+SCRATCH = {
+    "kv":   ("sbuf", [128, NB * BW], "bfloat16"),
+    "qs":   ("sbuf", [128, 128], "bfloat16"),
+    "z":    ("sbuf", [128, 129], "bfloat16"),
+    "dz":   ("dram", [129, 128], "bfloat16"),
+    "eye":  ("sbuf", [128, 128], "bfloat16"),
+    "zero": ("sbuf", [128, 128], "float32"),
+    "neg":  ("sbuf", [128, 128], "bfloat16"),
+    "acc":  ("sbuf", [128, 128], "float32"),
+    "tr":   ("sbuf", [128, 128], "float32"),
+    "mcol": ("sbuf", [128, 8], "bfloat16"),
+    "row":  ("sbuf", [128, 128], "bfloat16"),
+    "p":    ("sbuf", [128, NB * 128], "bfloat16"),
+    "yo":   ("sbuf", [128, 128], "bfloat16"),
+    "s0":   ("psum", [128, 512], "float32"),
+    "s1":   ("psum", [128, 512], "float32"),
+    "s2":   ("psum", [128, 512], "float32"),
+    "s3":   ("psum", [128, 512], "float32"),
+    "s4":   ("psum", [128, 512], "float32"),
+    "t0":   ("psum", [128, 512], "float32"),
+    "t1":   ("psum", [128, 512], "float32"),
+    "py":   ("psum", [128, 512], "float32"),
+}
+SEMAPHORES = (["ld", "ldq", "snd", "vs", "idz", "idi", "tt", "yl", "sto"]
+              + ["a%d" % j for j in range(NB)] + ["st%d" % j for j in range(NB)] + ["b%d" % j for j in range(NB)])
+
+
+def _plan(cores, wid, topo):
+    n = len(cores)
+
+    def site(r):
+        return (topo.host(cores[r]), topo.chip(cores[r]))
+
+    def near(a, b):
+        return a != b and topo.may_write(cores[a], cores[b])
+
+    first = {r: [] for r in range(n)}
+    second = {r: [] for r in range(n)}
+    load = [0] * n
+    used = {}
+    for j in range(n):
+        seen = []
+        for d in range(n):
+            if not near(j, d):
+                continue
+            if site(d) == site(j):
+                first[j].append(d)
+            elif site(d) not in seen:
+                seen.append(site(d))
+                mem = [x for x in range(n) if site(x) == site(d)]
+                port = mem[used.get(site(d), 0) % len(mem)]
+                used[site(d)] = used.get(site(d), 0) + 1
+                first[j].append(port)
+                load[j] += 1
+                for x in mem:
+                    if x != port:
+                        second[port].append((j, x))
+    far = [(j, d) for j in range(n) for d in range(n) if j != d and not near(j, d)]
+    far.sort(key=lambda p: -wid[p[1]])
+    for j, d in far:
+        cand = [x for x in first[j] if near(x, d) and site(x) != site(j)]
+        x = min(cand, key=lambda c: (load[c], -c))
+        load[x] += 1
+        second[x].append((j, d))
+    for x in range(n):
+        second[x].sort(key=lambda p: -wid[p[1]])
+
+    def urgency(j, x):
+        return max([wid[d] for (b, d) in second[x] if b == j] + [0])
+
+    sends = {}
+    for j in range(n):
+        f = sorted(first[j], key=lambda x: (site(x) == site(j), -urgency(j, x)))
+        sends[j] = [(j, x) for x in f] + second[j]
+    order = {}
+    for d in range(n):
+        pos = {}
+        for x in range(n):
+            for p, (b, t) in enumerate(sends[x]):
+                if t == d:
+                    pos[b] = (p, b != x, site(x) != site(d))
+        order[d] = [d] + sorted(pos, key=lambda b: pos[b])
+    return sends, order
+
+
+def _count(mask):
+    return bin(mask).count("1")
+
+
+def rank_program(g, core, T, topo):
+    rank = T.rank_of(core)
+    if rank is None:
+        return
+    cores = list(T.cores)
+    wid = list(T.tables["WID"])
+    sends, order = _plan(cores, wid, topo)
+    C = wid[rank]
+    sem = T.sem
+    te, ve = g.tensor, g.vector
+
+    def kblk(j):
+        return T.kv[:, j * BW:j * BW + 128]
+
+    def vblk(j):
+        return T.kv[:, j * BW + 128:(j + 1) * BW]
+
+    def mask_for(src, dst):
+        m = topo.mask(cores[src], cores[dst])
+        away = 0
+        for x in range(len(cores)):
+            mx = topo.mask(cores[src], cores[x]) if x != src else 0
+            if mx and mx != m and _count(mx) < _count(m):
+                away |= mx
+        rest = m & ~away
+        return rest if _count(rest) in (1, 2, 4, 8, 16) else m
+
+    need = {}
+    for x in range(len(cores)):
+        for (b, d) in sends[x]:
+            if d == rank:
+                need[b] = _count(mask_for(x, d))
+
+    g.sync.dma_start(kblk(rank), T.k[:, :]).then_inc(sem.ld, 16)
+    g.scalar.dma_start(vblk(rank), T.v[:, :]).then_inc(sem.ld, 16)
+    g.sync.dma_start(T.qs[:, 0:C], T.q[:, 0:C]).then_inc(sem.ldq, 16)
+
+    g.wait_ge(sem.ld, 32)
+    sent = 0
+    waited = {rank}
+    for (b, d) in sends[rank]:
+        if b not in waited:
+            g.wait_ge(sem["a%d" % b], need[b])
+            waited.add(b)
+        rid, pid = topo.addr(cores[d], core)
+        m = mask_for(rank, d)
+        blk = T.kv[:, b * BW:(b + 1) * BW]
+        g.remote_dma(out_ap=blk, in_ap=blk, remote_sem=sem["a%d" % b], local_sem=sem.snd,
+                     pid=pid, routing_id=rid, dma_engine_mask=m)
+        sent += _count(m)
+    g.wait_ge(sem.snd, sent)
+
+    nv = [0]
+
+    def chain():
+        if nv[0]:
+            ve.wait_ge(sem.vs, nv[0])
+
+    def done(ins):
+        ins.then_inc(sem.vs, 1)
+        nv[0] += 1
+        return nv[0]
+
+    chain(); done(ve.memset(T.z[:, :], 0.0))
+    chain(); z_ready = done(ve.memset(T.z[:, 0:1], 1.0))
+    chain(); done(ve.memset(T.zero[:, 0:C], 0.0))
+    chain(); done(ve.memset(T.neg[0:1, :], -0.5))
+
+    g.scalar.wait_ge(sem.vs, z_ready)
+    g.scalar.dma_start(T.dz[:, :], T.z[:, :]).then_inc(sem.idz, 16)
+    g.scalar.wait_ge(sem.idz, 16)
+    g.scalar.dma_start(T.eye[:, :], T.dz[0:128, :]).then_inc(sem.idi, 16)
+
+    sbank = [T.s0, T.s1, T.s2, T.s3, T.s4]
+    tbank = [T.t0, T.t1]
+    te.wait_ge(sem.ld, 32)
+    te.wait_ge(sem.ldq, 16)
+    acc_done = []
+    for i, j in enumerate(order[rank]):
+        if j != rank:
+            te.wait_ge(sem["a%d" % j], need[j])
+        if i >= 2:
+            te.wait_ge(sem.vs, acc_done[i - 2])
+        tb = tbank[i % 2]
+        te.matmul(tb[0:C, 0:128], T.qs[:, 0:C], kblk(j), True, True).then_inc(sem["st%d" % i], 1)
+        te.matmul(sbank[i][:, 0:C], kblk(j), T.qs[:, 0:C], True, False)
+        chain()
+        ve.wait_ge(sem["st%d" % i], 1)
+        if i == 0:
+            acc_done.append(done(ve.tensor_copy(T.acc[0:C, :], tb[0:C, 0:128])))
+        else:
+            acc_done.append(done(ve.tensor_tensor(T.acc[0:C, :], T.acc[0:C, :], tb[0:C, 0:128], AluOpType.max)))
+
+    chain(); done(ve.tensor_tensor(T.tr[0:C, 0:64], T.acc[0:C, 0:64], T.acc[0:C, 64:128], AluOpType.max))
+    base, w = 0, 64
+    while w > 2:
+        h = w // 2
+        chain()
+        done(ve.tensor_tensor(T.tr[0:C, base + w:base + w + h], T.tr[0:C, base:base + h],
+                              T.tr[0:C, base + h:base + w], AluOpType.max))
+        base, w = base + w, h
+    chain()
+    m_ready = done(ve.tensor_tensor(T.mcol[0:C, 0:1], T.tr[0:C, base:base + 1], T.tr[0:C, base + 1:base + 2],
+                                    AluOpType.max))
+
+    te.wait_ge(sem.vs, m_ready)
+    te.wait_ge(sem.idi, 16)
+    te.matmul(T.py[0:1, 128:128 + C], T.mcol[0:C, 0:1], T.eye[0:C, 0:C], True, True).then_inc(sem.tt, 1)
+    chain()
+    ve.wait_ge(sem.tt, 1)
+    row_ready = done(ve.tensor_copy(T.row[0:1, 0:C], T.py[0:1, 128:128 + C]))
+    te.wait_ge(sem.vs, row_ready)
+    for i in range(NB):
+        te.matmul(sbank[i][:, 0:C], T.neg[0:1, 0:128], T.row[0:1, 0:C], False, True).then_inc(sem["b%d" % i], 1)
+
+    for i, j in enumerate(order[rank]):
+        chain()
+        ve.wait_ge(sem["b%d" % i], 1)
+        p_ready = done(ve.tensor_tensor(T.p[:, i * 128:i * 128 + C], sbank[i][:, 0:C], T.zero[:, 0:C], AluOpType.max))
+        te.wait_ge(sem.vs, p_ready)
+        ins = te.matmul(T.py[:, 0:C], vblk(j), T.p[:, i * 128:i * 128 + C], i == 0, i == NB - 1)
+        if i == NB - 1:
+            ins.then_inc(sem.yl, 1)
+    chain()
+    ve.wait_ge(sem.yl, 1)
+    y_ready = done(ve.tensor_copy(T.yo[:, 0:C], T.py[:, 0:C]))
+
+    g.sync.wait_ge(sem.vs, y_ready)
+    g.sync.dma_start(T.y[:, 0:C], T.yo[:, 0:C]).then_inc(sem.sto, 16)
+    g.sync.wait_ge(sem.sto, 16)

@@ -1,20 +1,18 @@
-from concourse.mybir import AluOpType
+from concourse.mybir import AluOpType, AxisListType, ActivationFunctionType
 
 NB = 5
 BW = 256
+TOTAL = 512
 
 SCRATCH = {
     "kv":   ("sbuf", [128, NB * BW], "bfloat16"),
     "qs":   ("sbuf", [128, 128], "bfloat16"),
-    "z":    ("sbuf", [128, 129], "bfloat16"),
-    "dz":   ("dram", [129, 128], "bfloat16"),
+    "one":  ("sbuf", [128, 128], "bfloat16"),
     "eye":  ("sbuf", [128, 128], "bfloat16"),
-    "zero": ("sbuf", [128, 128], "float32"),
     "neg":  ("sbuf", [128, 128], "bfloat16"),
-    "acc":  ("sbuf", [128, 128], "float32"),
-    "tr":   ("sbuf", [128, 128], "float32"),
-    "mcol": ("sbuf", [128, 8], "bfloat16"),
-    "row":  ("sbuf", [128, 128], "bfloat16"),
+    "mx":   ("sbuf", [128, 8], "float32"),
+    "mm":   ("sbuf", [128, 4], "float32"),
+    "dg":   ("sbuf", [128, 128], "bfloat16"),
     "p":    ("sbuf", [128, NB * 128], "bfloat16"),
     "yo":   ("sbuf", [128, 128], "bfloat16"),
     "s0":   ("psum", [128, 512], "float32"),
@@ -26,65 +24,124 @@ SCRATCH = {
     "t1":   ("psum", [128, 512], "float32"),
     "py":   ("psum", [128, 512], "float32"),
 }
-SEMAPHORES = (["ld", "ldq", "snd", "vs", "idz", "idi", "tt", "yl", "sto"]
+SEMAPHORES = (["ld", "ldq", "snd", "vs", "idi", "yl", "sto"] + ["r%d" % j for j in range(NB)]
               + ["a%d" % j for j in range(NB)] + ["st%d" % j for j in range(NB)] + ["b%d" % j for j in range(NB)])
+
+_CACHE = {}
 
 
 def _plan(cores, wid, topo):
     n = len(cores)
 
-    def site(r):
-        return (topo.host(cores[r]), topo.chip(cores[r]))
+    def site(c):
+        return (topo.host(c), topo.chip(c))
 
-    def near(a, b):
-        return a != b and topo.may_write(cores[a], cores[b])
+    def ok(a, b):
+        return a != b and topo.may_write(a, b)
 
-    first = {r: [] for r in range(n)}
-    second = {r: [] for r in range(n)}
-    load = [0] * n
-    used = {}
+    top = max(wid)
+    spare = {}
+
+    def take(x, dests):
+        s = site(x)
+        if s not in spare:
+            spare[s] = [c for c in range(TOTAL) if site(c) == s and topo.die(c) == topo.die(x) and c not in cores]
+        for c in reversed(spare[s]):
+            if all(ok(c, t) for t in dests):
+                spare[s].remove(c)
+                return c
+        return None
+
+    first = {j: [] for j in range(n)}
+    second = {c: [] for c in cores}
+    served = set()
+    helpers = {}
+    direct = {j: [] for j in range(n)}
+
+    for d in range(n):
+        if wid[d] != top:
+            continue
+        for j in range(n):
+            if j == d or ok(cores[j], cores[d]):
+                continue
+            cand = [x for x in range(n) if ok(cores[j], cores[x]) and ok(cores[x], cores[d])
+                    and site(cores[x]) not in (site(cores[j]), site(cores[d]))]
+            x = min(cand, key=lambda c: (helpers.get(site(cores[c]), 0), c))
+            helpers[site(cores[x])] = helpers.get(site(cores[x]), 0) + 1
+            loc = [y for y in range(n) if site(cores[y]) == site(cores[x])]
+            h = take(cores[x], [cores[d]] + [cores[y] for y in loc])
+            first[j].append(h)
+            second[h] = [(j, cores[d])] + [(j, cores[y]) for y in loc]
+            served.add((j, d))
+            served.update((j, y) for y in loc)
+
     for j in range(n):
         seen = []
         for d in range(n):
-            if not near(j, d):
+            s = site(cores[d])
+            if s in seen:
                 continue
-            if site(d) == site(j):
-                first[j].append(d)
-            elif site(d) not in seen:
-                seen.append(site(d))
-                mem = [x for x in range(n) if site(x) == site(d)]
-                port = mem[used.get(site(d), 0) % len(mem)]
-                used[site(d)] = used.get(site(d), 0) + 1
-                first[j].append(port)
-                load[j] += 1
-                for x in mem:
-                    if x != port:
-                        second[port].append((j, x))
-    far = [(j, d) for j in range(n) for d in range(n) if j != d and not near(j, d)]
-    far.sort(key=lambda p: -wid[p[1]])
-    for j, d in far:
-        cand = [x for x in first[j] if near(x, d) and site(x) != site(j)]
-        x = min(cand, key=lambda c: (load[c], -c))
-        load[x] += 1
-        second[x].append((j, d))
-    for x in range(n):
-        second[x].sort(key=lambda p: -wid[p[1]])
+            seen.append(s)
+            mem = [x for x in range(n) if site(cores[x]) == s and x != j and (j, x) not in served
+                   and ok(cores[j], cores[x])]
+            if not mem:
+                continue
+            if s == site(cores[j]):
+                first[j] += [cores[x] for x in mem]
+            else:
+                e = max(mem, key=lambda x: wid[x])
+                first[j].append(cores[e])
+                direct[j].append(e)
+                second[cores[e]] += [(j, cores[x]) for x in mem if x != e]
+            served.update((j, x) for x in mem)
 
-    def urgency(j, x):
-        return max([wid[d] for (b, d) in second[x] if b == j] + [0])
+    def away(c, lst):
+        return len([t for t in lst if site(t) != site(c)])
 
-    sends = {}
     for j in range(n):
-        f = sorted(first[j], key=lambda x: (site(x) == site(j), -urgency(j, x)))
-        sends[j] = [(j, x) for x in f] + second[j]
-    order = {}
-    for d in range(n):
-        pos = {}
-        for x in range(n):
-            for p, (b, t) in enumerate(sends[x]):
-                if t == d:
-                    pos[b] = (p, b != x, site(x) != site(d))
-        order[d] = [d] + sorted(pos, key=lambda b: pos[b])
+        for d in range(n):
+            if j == d or (j, d) in served:
+                continue
+            cand = [x for x in direct[j] if ok(cores[x], cores[d])]
+            x = min(cand, key=lambda c: (away(cores[c], first[c]) + away(cores[c], [t for _, t in second[cores[c]]]), c))
+            second[cores[x]].append((j, cores[d]))
+            served.add((j, d))
+
+    def kind(j, t):
+        if site(t) == site(cores[j]):
+            return 3
+        if t not in cores:
+            return 0
+        return 1 if any(b == j and site(u) != site(t) for b, u in second[t]) else 2
+
+    own = {cores[j]: [(j, t) for t in sorted(first[j], key=lambda t: kind(j, t))] for j in range(n)}
+
+    def estimate(lists):
+        arr = {(j, cores[j]): 0.0 for j in range(n)}
+        for _ in range(6):
+            for c, lst in lists.items():
+                t = 0.0
+                free = {True: 0.0, False: 0.0}
+                fresh = 0.5
+                for b, u in lst:
+                    if (b, c) not in arr:
+                        break
+                    t = max(t, arr[(b, c)] + (0.0 if c in cores and cores.index(c) == b else 0.3))
+                    on = site(u) == site(c)
+                    st = max(t, free[on]) + fresh
+                    fresh = 0.0
+                    free[on] = st + 1.0
+                    arr[(b, u)] = st + 1.0
+                    t += 0.05
+        return arr
+
+    sends = {c: own.get(c, []) + second[c] for c in second}
+    for _ in range(2):
+        arr = estimate(sends)
+        sends = {c: own.get(c, []) + sorted(second[c], key=lambda p: (arr[(p[0], c)], site(p[1]) == site(c)))
+                 for c in second}
+    arr = estimate(sends)
+    order = {d: sorted(range(n), key=lambda b: arr[(b, cores[d])]) for d in range(n)}
     return sends, order
 
 
@@ -93,15 +150,57 @@ def _count(mask):
 
 
 def rank_program(g, core, T, topo):
-    rank = T.rank_of(core)
-    if rank is None:
-        return
     cores = list(T.cores)
     wid = list(T.tables["WID"])
-    sends, order = _plan(cores, wid, topo)
-    C = wid[rank]
+    if "plan" not in _CACHE:
+        _CACHE["plan"] = _plan(cores, wid, topo)
+    sends, order = _CACHE["plan"]
+    if core not in sends:
+        return
+    rank = T.rank_of(core)
     sem = T.sem
-    te, ve = g.tensor, g.vector
+
+    def same_chip(a, b):
+        return (topo.host(a), topo.chip(a)) == (topo.host(b), topo.chip(b))
+
+    def mask_for(src, dst):
+        m = topo.mask(src, dst)
+        if not same_chip(src, dst):
+            return m
+        away = 0
+        for x in cores:
+            if x != src and not same_chip(src, x):
+                away |= topo.mask(src, x)
+        rest = m & ~away
+        return rest if _count(rest) in (1, 2, 4, 8, 16) else m
+
+    need = {}
+    for x in sends:
+        for (b, d) in sends[x]:
+            if d == core:
+                need[b] = _count(mask_for(x, d))
+
+    def gather(have):
+        sent = 0
+        waited = set(have)
+        for (b, d) in sends[core]:
+            if b not in waited:
+                g.wait_ge(sem["a%d" % b], need[b])
+                waited.add(b)
+            rid, pid = topo.addr(d, core)
+            m = mask_for(core, d)
+            blk = T.kv[:, b * BW:(b + 1) * BW]
+            g.remote_dma(out_ap=blk, in_ap=blk, remote_sem=sem["a%d" % b], local_sem=sem.snd,
+                         pid=pid, routing_id=rid, dma_engine_mask=m)
+            sent += _count(m)
+        g.wait_ge(sem.snd, sent)
+
+    if rank is None:
+        gather([])
+        return
+
+    C = wid[rank]
+    te, ve, ac = g.tensor, g.vector, g.scalar
 
     def kblk(j):
         return T.kv[:, j * BW:j * BW + 128]
@@ -109,40 +208,9 @@ def rank_program(g, core, T, topo):
     def vblk(j):
         return T.kv[:, j * BW + 128:(j + 1) * BW]
 
-    def mask_for(src, dst):
-        m = topo.mask(cores[src], cores[dst])
-        away = 0
-        for x in range(len(cores)):
-            mx = topo.mask(cores[src], cores[x]) if x != src else 0
-            if mx and mx != m and _count(mx) < _count(m):
-                away |= mx
-        rest = m & ~away
-        return rest if _count(rest) in (1, 2, 4, 8, 16) else m
-
-    need = {}
-    for x in range(len(cores)):
-        for (b, d) in sends[x]:
-            if d == rank:
-                need[b] = _count(mask_for(x, d))
-
     g.sync.dma_start(kblk(rank), T.k[:, :]).then_inc(sem.ld, 16)
     g.scalar.dma_start(vblk(rank), T.v[:, :]).then_inc(sem.ld, 16)
     g.sync.dma_start(T.qs[:, 0:C], T.q[:, 0:C]).then_inc(sem.ldq, 16)
-
-    g.wait_ge(sem.ld, 32)
-    sent = 0
-    waited = {rank}
-    for (b, d) in sends[rank]:
-        if b not in waited:
-            g.wait_ge(sem["a%d" % b], need[b])
-            waited.add(b)
-        rid, pid = topo.addr(cores[d], core)
-        m = mask_for(rank, d)
-        blk = T.kv[:, b * BW:(b + 1) * BW]
-        g.remote_dma(out_ap=blk, in_ap=blk, remote_sem=sem["a%d" % b], local_sem=sem.snd,
-                     pid=pid, routing_id=rid, dma_engine_mask=m)
-        sent += _count(m)
-    g.wait_ge(sem.snd, sent)
 
     nv = [0]
 
@@ -155,64 +223,51 @@ def rank_program(g, core, T, topo):
         nv[0] += 1
         return nv[0]
 
-    chain(); done(ve.memset(T.z[:, :], 0.0))
-    chain(); z_ready = done(ve.memset(T.z[:, 0:1], 1.0))
-    chain(); done(ve.memset(T.zero[:, 0:C], 0.0))
-    chain(); done(ve.memset(T.neg[0:1, :], -0.5))
+    one_ready = done(ve.memset(T.one[0:C, 0:C], 1.0))
+    chain(); done(ve.memset(T.neg[0:C, :], -0.5))
 
-    g.scalar.wait_ge(sem.vs, z_ready)
-    g.scalar.dma_start(T.dz[:, :], T.z[:, :]).then_inc(sem.idz, 16)
-    g.scalar.wait_ge(sem.idz, 16)
-    g.scalar.dma_start(T.eye[:, :], T.dz[0:128, :]).then_inc(sem.idi, 16)
+    g.wait_ge(sem.vs, one_ready)
+    g.affine_select(T.eye[0:C, 0:C], T.one[0:C, 0:C], [[-1, C]], AluOpType.is_equal, 0.0, 0, 1).then_inc(sem.idi, 1)
+
+    g.wait_ge(sem.ld, 32)
+    gather([rank])
 
     sbank = [T.s0, T.s1, T.s2, T.s3, T.s4]
     tbank = [T.t0, T.t1]
     te.wait_ge(sem.ld, 32)
     te.wait_ge(sem.ldq, 16)
-    acc_done = []
+    red_done = []
     for i, j in enumerate(order[rank]):
         if j != rank:
             te.wait_ge(sem["a%d" % j], need[j])
         if i >= 2:
-            te.wait_ge(sem.vs, acc_done[i - 2])
+            te.wait_ge(sem.vs, red_done[i - 2])
         tb = tbank[i % 2]
         te.matmul(tb[0:C, 0:128], T.qs[:, 0:C], kblk(j), True, True).then_inc(sem["st%d" % i], 1)
         te.matmul(sbank[i][:, 0:C], kblk(j), T.qs[:, 0:C], True, False)
         chain()
         ve.wait_ge(sem["st%d" % i], 1)
-        if i == 0:
-            acc_done.append(done(ve.tensor_copy(T.acc[0:C, :], tb[0:C, 0:128])))
-        else:
-            acc_done.append(done(ve.tensor_tensor(T.acc[0:C, :], T.acc[0:C, :], tb[0:C, 0:128], AluOpType.max)))
+        red_done.append(done(ve.tensor_reduce(T.mx[0:C, i:i + 1], tb[0:C, 0:128], AxisListType.X, AluOpType.max)))
 
-    chain(); done(ve.tensor_tensor(T.tr[0:C, 0:64], T.acc[0:C, 0:64], T.acc[0:C, 64:128], AluOpType.max))
-    base, w = 0, 64
-    while w > 2:
-        h = w // 2
-        chain()
-        done(ve.tensor_tensor(T.tr[0:C, base + w:base + w + h], T.tr[0:C, base:base + h],
-                              T.tr[0:C, base + h:base + w], AluOpType.max))
-        base, w = base + w, h
+    chain(); done(ve.tensor_reduce(T.mm[0:C, 0:1], T.mx[0:C, 0:NB], AxisListType.X, AluOpType.max))
     chain()
-    m_ready = done(ve.tensor_tensor(T.mcol[0:C, 0:1], T.tr[0:C, base:base + 1], T.tr[0:C, base + 1:base + 2],
-                                    AluOpType.max))
-
-    te.wait_ge(sem.vs, m_ready)
-    te.wait_ge(sem.idi, 16)
-    te.matmul(T.py[0:1, 128:128 + C], T.mcol[0:C, 0:1], T.eye[0:C, 0:C], True, True).then_inc(sem.tt, 1)
-    chain()
-    ve.wait_ge(sem.tt, 1)
-    row_ready = done(ve.tensor_copy(T.row[0:1, 0:C], T.py[0:1, 128:128 + C]))
-    te.wait_ge(sem.vs, row_ready)
+    ve.wait_ge(sem.idi, 1)
+    d_ready = done(ve.tensor_scalar(T.dg[0:C, 0:C], T.eye[0:C, 0:C], T.mm[0:C, 0:1], None, AluOpType.mult))
+    te.wait_ge(sem.vs, d_ready)
     for i in range(NB):
-        te.matmul(sbank[i][:, 0:C], T.neg[0:1, 0:128], T.row[0:1, 0:C], False, True).then_inc(sem["b%d" % i], 1)
+        te.matmul(sbank[i][:, 0:C], T.neg[0:C, 0:128], T.dg[0:C, 0:C], False, True).then_inc(sem["b%d" % i], 1)
 
     for i, j in enumerate(order[rank]):
-        chain()
-        ve.wait_ge(sem["b%d" % i], 1)
-        p_ready = done(ve.tensor_tensor(T.p[:, i * 128:i * 128 + C], sbank[i][:, 0:C], T.zero[:, 0:C], AluOpType.max))
-        te.wait_ge(sem.vs, p_ready)
-        ins = te.matmul(T.py[:, 0:C], vblk(j), T.p[:, i * 128:i * 128 + C], i == 0, i == NB - 1)
+        pj = T.p[:, i * 128:i * 128 + C]
+        if i % 2 == 0:
+            chain()
+            ve.wait_ge(sem["b%d" % i], 1)
+            te.wait_ge(sem.vs, done(ve.tensor_scalar(pj, sbank[i][:, 0:C], 0.0, None, AluOpType.max)))
+        else:
+            ac.wait_ge(sem["b%d" % i], 1)
+            ac.activation(pj, sbank[i][:, 0:C], ActivationFunctionType.Relu).then_inc(sem["r%d" % i], 1)
+            te.wait_ge(sem["r%d" % i], 1)
+        ins = te.matmul(T.py[:, 0:C], vblk(j), pj, i == 0, i == NB - 1)
         if i == NB - 1:
             ins.then_inc(sem.yl, 1)
     chain()

@@ -1,3 +1,4 @@
+from concourse.bass import DstId, RemoteDMATransfer
 from concourse.mybir import AluOpType, AxisListType, ActivationFunctionType
 
 NB = 5
@@ -5,6 +6,8 @@ BW = 256
 TOTAL = 512
 
 SCRATCH = {
+    "kd":   ("dram", [128, 128], "bfloat16"),
+    "vd":   ("dram", [128, 128], "bfloat16"),
     "kv":   ("sbuf", [128, NB * BW], "bfloat16"),
     "qs":   ("sbuf", [128, 128], "bfloat16"),
     "one":  ("sbuf", [128, 128], "bfloat16"),
@@ -24,8 +27,9 @@ SCRATCH = {
     "t1":   ("psum", [128, 512], "float32"),
     "py":   ("psum", [128, 512], "float32"),
 }
-SEMAPHORES = (["ld", "ldq", "snd", "vs", "idi", "yl", "sto"] + ["r%d" % j for j in range(NB)]
-              + ["a%d" % j for j in range(NB)] + ["st%d" % j for j in range(NB)] + ["b%d" % j for j in range(NB)])
+SEMAPHORES = (["ldk", "ldv", "ld", "ldq", "h1", "snd", "vs", "idi", "yl", "sto"] + ["r%d" % j for j in range(NB)]
+              + ["a%d" % j for j in range(NB)] + ["c%d" % j for j in range(NB)]
+              + ["st%d" % j for j in range(NB)] + ["b%d" % j for j in range(NB)])
 
 _CACHE = {}
 
@@ -39,7 +43,6 @@ def _plan(cores, wid, topo):
     def ok(a, b):
         return a != b and topo.may_write(a, b)
 
-    top = max(wid)
     spare = {}
 
     def take(x, dests):
@@ -52,97 +55,57 @@ def _plan(cores, wid, topo):
                 return c
         return None
 
-    first = {j: [] for j in range(n)}
-    second = {c: [] for c in cores}
-    served = set()
-    helpers = {}
+    at = {}
+    for x in range(n):
+        at.setdefault(site(cores[x]), []).append(x)
+    hop1 = {j: [] for j in range(n)}
+    fwd = {}
     direct = {j: [] for j in range(n)}
-
-    for d in range(n):
-        if wid[d] != top:
-            continue
-        for j in range(n):
-            if j == d or ok(cores[j], cores[d]):
-                continue
-            cand = [x for x in range(n) if ok(cores[j], cores[x]) and ok(cores[x], cores[d])
-                    and site(cores[x]) not in (site(cores[j]), site(cores[d]))]
-            x = min(cand, key=lambda c: (helpers.get(site(cores[c]), 0), c))
-            helpers[site(cores[x])] = helpers.get(site(cores[x]), 0) + 1
-            loc = [y for y in range(n) if site(cores[y]) == site(cores[x])]
-            h = take(cores[x], [cores[d]] + [cores[y] for y in loc])
-            first[j].append(h)
-            second[h] = [(j, cores[d])] + [(j, cores[y]) for y in loc]
-            served.add((j, d))
-            served.update((j, y) for y in loc)
-
+    onchip = {j: [] for j in range(n)}
+    relay = {c: [] for c in cores}
+    busy = {}
     for j in range(n):
-        seen = []
-        for d in range(n):
-            s = site(cores[d])
-            if s in seen:
+        o = cores[j]
+        far = sorted([d for d in range(n) if d != j and not ok(o, cores[d])], key=lambda d: -wid[d])
+        used = []
+        for d in far:
+            cand = [s for s in at if s not in used and s not in (site(o), site(cores[d]))
+                    and all(ok(o, cores[x]) and ok(cores[x], cores[d]) for x in at[s])]
+            s = min(cand, key=lambda s: (len(at[s]), busy.get(s, 0), topo.rack(s[0]) != topo.rack(topo.host(o)), s))
+            used.append(s)
+            busy[s] = busy.get(s, 0) + 1
+            dests = sorted([d] + at[s], key=lambda x: -wid[x])
+            h = take(cores[at[s][0]], [cores[x] for x in dests])
+            hop1[j].append(h)
+            fwd[h] = (j, [cores[x] for x in dests])
+        for s in at:
+            mem = [x for x in at[s] if x != j]
+            if s in used or not mem or not ok(o, cores[mem[0]]):
                 continue
-            seen.append(s)
-            mem = [x for x in range(n) if site(cores[x]) == s and x != j and (j, x) not in served
-                   and ok(cores[j], cores[x])]
-            if not mem:
-                continue
-            if s == site(cores[j]):
-                first[j] += [cores[x] for x in mem]
+            if s == site(o):
+                onchip[j] += [cores[x] for x in mem]
             else:
                 e = max(mem, key=lambda x: wid[x])
-                first[j].append(cores[e])
-                direct[j].append(e)
-                second[cores[e]] += [(j, cores[x]) for x in mem if x != e]
-            served.update((j, x) for x in mem)
+                direct[j].append(cores[e])
+                relay[cores[e]] += [(j, cores[x]) for x in mem if x != e]
 
-    def away(c, lst):
-        return len([t for t in lst if site(t) != site(c)])
-
+    arr = {}
     for j in range(n):
-        for d in range(n):
-            if j == d or (j, d) in served:
-                continue
-            cand = [x for x in direct[j] if ok(cores[x], cores[d])]
-            x = min(cand, key=lambda c: (away(cores[c], first[c]) + away(cores[c], [t for _, t in second[cores[c]]]), c))
-            second[cores[x]].append((j, cores[d]))
-            served.add((j, d))
-
-    def kind(j, t):
-        if site(t) == site(cores[j]):
-            return 3
-        if t not in cores:
-            return 0
-        return 1 if any(b == j and site(u) != site(t) for b, u in second[t]) else 2
-
-    own = {cores[j]: [(j, t) for t in sorted(first[j], key=lambda t: kind(j, t))] for j in range(n)}
-
-    def estimate(lists):
-        arr = {(j, cores[j]): 0.0 for j in range(n)}
-        for _ in range(6):
-            for c, lst in lists.items():
-                t = 0.0
-                free = {True: 0.0, False: 0.0}
-                fresh = 0.5
-                for b, u in lst:
-                    if (b, c) not in arr:
-                        break
-                    t = max(t, arr[(b, c)] + (0.0 if c in cores and cores.index(c) == b else 0.3))
-                    on = site(u) == site(c)
-                    st = max(t, free[on]) + fresh
-                    fresh = 0.0
-                    free[on] = st + 1.0
-                    arr[(b, u)] = st + 1.0
-                    t += 0.05
-        return arr
-
-    sends = {c: own.get(c, []) + second[c] for c in second}
-    for _ in range(2):
-        arr = estimate(sends)
-        sends = {c: own.get(c, []) + sorted(second[c], key=lambda p: (arr[(p[0], c)], site(p[1]) == site(c)))
-                 for c in second}
-    arr = estimate(sends)
+        arr[(j, cores[j])] = 0.0
+        for i, h in enumerate(hop1[j]):
+            for u, t in enumerate(fwd[h][1]):
+                arr[(j, t)] = 3.0 + 0.3 * i + 0.1 * u
+        for i, t in enumerate(direct[j]):
+            arr[(j, t)] = 2.0 + 0.3 * len(hop1[j]) + i
+            for b, u in relay[t]:
+                if b == j:
+                    arr[(j, u)] = arr[(j, t)] + 1.0
+        for t in onchip[j]:
+            arr[(j, t)] = 1.5
     order = {d: sorted(range(n), key=lambda b: arr[(b, cores[d])]) for d in range(n)}
-    return sends, order
+    for c in relay:
+        relay[c].sort(key=lambda p: arr[(p[0], c)])
+    return hop1, fwd, direct, onchip, relay, order
 
 
 def _count(mask):
@@ -154,10 +117,10 @@ def rank_program(g, core, T, topo):
     wid = list(T.tables["WID"])
     if "plan" not in _CACHE:
         _CACHE["plan"] = _plan(cores, wid, topo)
-    sends, order = _CACHE["plan"]
-    if core not in sends:
-        return
+    hop1, fwd, direct, onchip, relay, order = _CACHE["plan"]
     rank = T.rank_of(core)
+    if rank is None and core not in fwd:
+        return
     sem = T.sem
 
     def same_chip(a, b):
@@ -174,33 +137,33 @@ def rank_program(g, core, T, topo):
         rest = m & ~away
         return rest if _count(rest) in (1, 2, 4, 8, 16) else m
 
-    need = {}
-    for x in sends:
-        for (b, d) in sends[x]:
-            if d == core:
-                need[b] = _count(mask_for(x, d))
+    def hop_masks(j):
+        hs = hop1[j]
+        if len(hs) == 1:
+            return [mask_for(cores[j], hs[0])]
+        bits = [i for i in range(16) if all((topo.mask(cores[j], h) >> i) & 1 for h in hs)]
+        size = 1
+        while size * 2 * len(hs) <= len(bits):
+            size *= 2
+        return [sum(1 << i for i in bits[u * size:(u + 1) * size]) for u in range(len(hs))]
 
-    def gather(have):
-        sent = 0
-        waited = set(have)
-        for (b, d) in sends[core]:
-            if b not in waited:
-                g.wait_ge(sem["a%d" % b], need[b])
-                waited.add(b)
+    def fused(dsts, masks, out_ap, in_ap, rsem, lsem):
+        trs = []
+        for d, m in zip(dsts, masks):
             rid, pid = topo.addr(d, core)
-            m = mask_for(core, d)
-            blk = T.kv[:, b * BW:(b + 1) * BW]
-            g.remote_dma(out_ap=blk, in_ap=blk, remote_sem=sem["a%d" % b], local_sem=sem.snd,
-                         pid=pid, routing_id=rid, dma_engine_mask=m)
-            sent += _count(m)
-        g.wait_ge(sem.snd, sent)
+            trs.append(RemoteDMATransfer(dst_ids=[DstId(rid=rid, pnc=pid)], dma_engine_mask=m, remote_sem=rsem,
+                                         src=in_ap, dst=out_ap))
+        g.remote_dma_fused(trs, local_sem=lsem)
+        return sum(_count(m) for m in masks)
 
-    if rank is None:
-        gather([])
-        return
+    def hands_on(c, b):
+        return any(x == b for x, _ in relay[c])
 
-    C = wid[rank]
-    te, ve, ac = g.tensor, g.vector, g.scalar
+    def send(dst, out_ap, in_ap, rsem, lsem, m):
+        rid, pid = topo.addr(dst, core)
+        g.remote_dma(out_ap=out_ap, in_ap=in_ap, remote_sem=rsem, local_sem=lsem,
+                     pid=pid, routing_id=rid, dma_engine_mask=m)
+        return _count(m)
 
     def kblk(j):
         return T.kv[:, j * BW:j * BW + 128]
@@ -208,9 +171,38 @@ def rank_program(g, core, T, topo):
     def vblk(j):
         return T.kv[:, j * BW + 128:(j + 1) * BW]
 
+    if rank is None:
+        b, dests = fwd[core]
+        got = _count(hop_masks(b)[hop1[b].index(core)])
+        sent = 0
+        for name, buf, slot in (("a%d" % b, T.kd, kblk(b)), ("c%d" % b, T.vd, vblk(b))):
+            g.wait_ge(sem[name], got)
+            sent += fused(dests, [mask_for(core, d) for d in dests], slot, buf[:, :], sem[name], sem.snd)
+        g.wait_ge(sem.snd, sent)
+        return
+
+    need = {}
+    for h in fwd:
+        if core in fwd[h][1]:
+            c = _count(mask_for(h, core))
+            need[fwd[h][0]] = (c, c)
+    for j in range(NB):
+        if core in direct[j] or core in onchip[j]:
+            c = _count(mask_for(cores[j], core))
+            need[j] = (c, c if hands_on(core, j) else None)
+    for x in relay:
+        for (b, d) in relay[x]:
+            if d == core:
+                c = _count(topo.mask(x, d))
+                need[b] = (c, c)
+
+    C = wid[rank]
+    te, ve, ac = g.tensor, g.vector, g.scalar
+
+    g.sync.dma_start(T.kd[:, :], T.k[:, :]).then_inc(sem.ldk, 16)
+    g.scalar.dma_start(T.vd[:, :], T.v[:, :]).then_inc(sem.ldv, 16)
     g.sync.dma_start(kblk(rank), T.k[:, :]).then_inc(sem.ld, 16)
     g.scalar.dma_start(vblk(rank), T.v[:, :]).then_inc(sem.ld, 16)
-    g.sync.dma_start(T.qs[:, 0:C], T.q[:, 0:C]).then_inc(sem.ldq, 16)
 
     nv = [0]
 
@@ -226,11 +218,29 @@ def rank_program(g, core, T, topo):
     one_ready = done(ve.memset(T.one[0:C, 0:C], 1.0))
     chain(); done(ve.memset(T.neg[0:C, :], -0.5))
 
-    g.wait_ge(sem.vs, one_ready)
-    g.affine_select(T.eye[0:C, 0:C], T.one[0:C, 0:C], [[-1, C]], AluOpType.is_equal, 0.0, 0, 1).then_inc(sem.idi, 1)
+    left = 0
+    for lsem, buf, name in ((sem.ldk, T.kd, "a%d" % rank), (sem.ldv, T.vd, "c%d" % rank)):
+        g.wait_ge(lsem, 16)
+        left += fused(hop1[rank], hop_masks(rank), buf[:, :], buf[:, :], sem[name], sem.h1)
+    g.sync.wait_ge(sem.h1, left)
+    g.sync.dma_start(T.qs[:, 0:C], T.q[:, 0:C]).then_inc(sem.ldq, 16)
 
     g.wait_ge(sem.ld, 32)
-    gather([rank])
+    sent = 0
+    own = T.kv[:, rank * BW:(rank + 1) * BW]
+    for d in direct[rank] + onchip[rank]:
+        if hands_on(d, rank):
+            sent += send(d, kblk(rank), kblk(rank), sem["a%d" % rank], sem.snd, mask_for(core, d))
+            sent += send(d, vblk(rank), vblk(rank), sem["c%d" % rank], sem.snd, mask_for(core, d))
+        else:
+            sent += send(d, own, own, sem["a%d" % rank], sem.snd, mask_for(core, d))
+    g.wait_ge(sem.vs, one_ready)
+    g.affine_select(T.eye[0:C, 0:C], T.one[0:C, 0:C], [[-1, C]], AluOpType.is_equal, 0.0, 0, 1).then_inc(sem.idi, 1)
+    for half, name, part in ((0, "a%d", kblk), (1, "c%d", vblk)):
+        for (b, d) in relay[core]:
+            g.wait_ge(sem[name % b], need[b][half])
+            sent += send(d, part(b), part(b), sem[name % b], sem.snd, topo.mask(core, d))
+    g.wait_ge(sem.snd, sent)
 
     sbank = [T.s0, T.s1, T.s2, T.s3, T.s4]
     tbank = [T.t0, T.t1]
@@ -239,7 +249,7 @@ def rank_program(g, core, T, topo):
     red_done = []
     for i, j in enumerate(order[rank]):
         if j != rank:
-            te.wait_ge(sem["a%d" % j], need[j])
+            te.wait_ge(sem["a%d" % j], need[j][0])
         if i >= 2:
             te.wait_ge(sem.vs, red_done[i - 2])
         tb = tbank[i % 2]
@@ -267,6 +277,8 @@ def rank_program(g, core, T, topo):
             ac.wait_ge(sem["b%d" % i], 1)
             ac.activation(pj, sbank[i][:, 0:C], ActivationFunctionType.Relu).then_inc(sem["r%d" % i], 1)
             te.wait_ge(sem["r%d" % i], 1)
+        if j != rank and need[j][1] is not None:
+            te.wait_ge(sem["c%d" % j], need[j][1])
         ins = te.matmul(T.py[:, 0:C], vblk(j), pj, i == 0, i == NB - 1)
         if i == NB - 1:
             ins.then_inc(sem.yl, 1)

from concourse.bass import DstId, RemoteDMATransfer
from concourse.mybir import AluOpType, AxisListType, ActivationFunctionType

NB = 5
BW = 256
TOTAL = 512

SCRATCH = {
    "kd":   ("dram", [128, 128], "bfloat16"),
    "vd":   ("dram", [128, 128], "bfloat16"),
    "kv":   ("sbuf", [128, NB * BW], "bfloat16"),
    "qs":   ("sbuf", [128, 128], "bfloat16"),
    "one":  ("sbuf", [128, 128], "bfloat16"),
    "eye":  ("sbuf", [128, 128], "bfloat16"),
    "neg":  ("sbuf", [128, 128], "bfloat16"),
    "mx":   ("sbuf", [128, 8], "float32"),
    "mm":   ("sbuf", [128, 4], "float32"),
    "dg":   ("sbuf", [128, 128], "bfloat16"),
    "p":    ("sbuf", [128, NB * 128], "bfloat16"),
    "yo":   ("sbuf", [128, 128], "bfloat16"),
    "s0":   ("psum", [128, 512], "float32"),
    "s1":   ("psum", [128, 512], "float32"),
    "s2":   ("psum", [128, 512], "float32"),
    "s3":   ("psum", [128, 512], "float32"),
    "s4":   ("psum", [128, 512], "float32"),
    "t0":   ("psum", [128, 512], "float32"),
    "t1":   ("psum", [128, 512], "float32"),
    "py":   ("psum", [128, 512], "float32"),
}
SEMAPHORES = (["ldk", "ldv", "ld", "ldq", "h1", "snd", "vs", "idi", "yl", "sto"] + ["r%d" % j for j in range(NB)]
              + ["a%d" % j for j in range(NB)] + ["c%d" % j for j in range(NB)]
              + ["st%d" % j for j in range(NB)] + ["b%d" % j for j in range(NB)])

_CACHE = {}


def _plan(cores, wid, topo):
    n = len(cores)

    def site(c):
        return (topo.host(c), topo.chip(c))

    def ok(a, b):
        return a != b and topo.may_write(a, b)

    spare = {}

    def take(x, dests):
        s = site(x)
        if s not in spare:
            spare[s] = [c for c in range(TOTAL) if site(c) == s and topo.die(c) == topo.die(x) and c not in cores]
        for c in reversed(spare[s]):
            if all(ok(c, t) for t in dests):
                spare[s].remove(c)
                return c
        return None

    at = {}
    for x in range(n):
        at.setdefault(site(cores[x]), []).append(x)
    hop1 = {j: [] for j in range(n)}
    fwd = {}
    direct = {j: [] for j in range(n)}
    onchip = {j: [] for j in range(n)}
    relay = {c: [] for c in cores}
    busy = {}
    for j in range(n):
        o = cores[j]
        far = sorted([d for d in range(n) if d != j and not ok(o, cores[d])], key=lambda d: -wid[d])
        used = []
        for d in far:
            cand = [s for s in at if s not in used and s not in (site(o), site(cores[d]))
                    and all(ok(o, cores[x]) and ok(cores[x], cores[d]) for x in at[s])]
            s = min(cand, key=lambda s: (len(at[s]), busy.get(s, 0), topo.rack(s[0]) != topo.rack(topo.host(o)), s))
            used.append(s)
            busy[s] = busy.get(s, 0) + 1
            dests = sorted([d] + at[s], key=lambda x: -wid[x])
            h = take(cores[at[s][0]], [cores[x] for x in dests])
            hop1[j].append(h)
            fwd[h] = (j, [cores[x] for x in dests])
        for s in at:
            mem = [x for x in at[s] if x != j]
            if s in used or not mem or not ok(o, cores[mem[0]]):
                continue
            if s == site(o):
                onchip[j] += [cores[x] for x in mem]
            else:
                e = max(mem, key=lambda x: wid[x])
                direct[j].append(cores[e])
                relay[cores[e]] += [(j, cores[x]) for x in mem if x != e]

    arr = {}
    for j in range(n):
        arr[(j, cores[j])] = 0.0
        for i, h in enumerate(hop1[j]):
            for u, t in enumerate(fwd[h][1]):
                arr[(j, t)] = 3.0 + 0.3 * i + 0.1 * u
        for i, t in enumerate(direct[j]):
            arr[(j, t)] = 2.0 + 0.3 * len(hop1[j]) + i
            for b, u in relay[t]:
                if b == j:
                    arr[(j, u)] = arr[(j, t)] + 1.0
        for t in onchip[j]:
            arr[(j, t)] = 1.5
    order = {d: sorted(range(n), key=lambda b: arr[(b, cores[d])]) for d in range(n)}
    for c in relay:
        relay[c].sort(key=lambda p: arr[(p[0], c)])
    return hop1, fwd, direct, onchip, relay, order


def _count(mask):
    return bin(mask).count("1")


def rank_program(g, core, T, topo):
    cores = list(T.cores)
    wid = list(T.tables["WID"])
    if "plan" not in _CACHE:
        _CACHE["plan"] = _plan(cores, wid, topo)
    hop1, fwd, direct, onchip, relay, order = _CACHE["plan"]
    rank = T.rank_of(core)
    if rank is None and core not in fwd:
        return
    sem = T.sem

    def same_chip(a, b):
        return (topo.host(a), topo.chip(a)) == (topo.host(b), topo.chip(b))

    def mask_for(src, dst):
        m = topo.mask(src, dst)
        if not same_chip(src, dst):
            return m
        away = 0
        for x in cores:
            if x != src and not same_chip(src, x):
                away |= topo.mask(src, x)
        rest = m & ~away
        return rest if _count(rest) in (1, 2, 4, 8, 16) else m

    def hop_masks(j):
        hs = hop1[j]
        if len(hs) == 1:
            return [mask_for(cores[j], hs[0])]
        bits = [i for i in range(16) if all((topo.mask(cores[j], h) >> i) & 1 for h in hs)]
        size = 1
        while size * 2 * len(hs) <= len(bits):
            size *= 2
        return [sum(1 << i for i in bits[u * size:(u + 1) * size]) for u in range(len(hs))]

    def fused(dsts, masks, out_ap, in_ap, rsem, lsem):
        trs = []
        for d, m in zip(dsts, masks):
            rid, pid = topo.addr(d, core)
            trs.append(RemoteDMATransfer(dst_ids=[DstId(rid=rid, pnc=pid)], dma_engine_mask=m, remote_sem=rsem,
                                         src=in_ap, dst=out_ap))
        g.remote_dma_fused(trs, local_sem=lsem)
        return sum(_count(m) for m in masks)

    def hands_on(c, b):
        return any(x == b for x, _ in relay[c])

    def send(dst, out_ap, in_ap, rsem, lsem, m):
        rid, pid = topo.addr(dst, core)
        g.remote_dma(out_ap=out_ap, in_ap=in_ap, remote_sem=rsem, local_sem=lsem,
                     pid=pid, routing_id=rid, dma_engine_mask=m)
        return _count(m)

    def kblk(j):
        return T.kv[:, j * BW:j * BW + 128]

    def vblk(j):
        return T.kv[:, j * BW + 128:(j + 1) * BW]

    if rank is None:
        b, dests = fwd[core]
        got = _count(hop_masks(b)[hop1[b].index(core)])
        sent = 0
        for name, buf, slot in (("a%d" % b, T.kd, kblk(b)), ("c%d" % b, T.vd, vblk(b))):
            g.wait_ge(sem[name], got)
            sent += fused(dests, [mask_for(core, d) for d in dests], slot, buf[:, :], sem[name], sem.snd)
        g.wait_ge(sem.snd, sent)
        return

    need = {}
    for h in fwd:
        if core in fwd[h][1]:
            c = _count(mask_for(h, core))
            need[fwd[h][0]] = (c, c)
    for j in range(NB):
        if core in direct[j] or core in onchip[j]:
            c = _count(mask_for(cores[j], core))
            need[j] = (c, c if hands_on(core, j) else None)
    for x in relay:
        for (b, d) in relay[x]:
            if d == core:
                c = _count(topo.mask(x, d))
                need[b] = (c, c)

    C = wid[rank]
    te, ve, ac = g.tensor, g.vector, g.scalar

    g.sync.dma_start(T.kd[:, :], T.k[:, :]).then_inc(sem.ldk, 16)
    g.scalar.dma_start(T.vd[:, :], T.v[:, :]).then_inc(sem.ldv, 16)
    g.sync.dma_start(kblk(rank), T.k[:, :]).then_inc(sem.ld, 16)
    g.scalar.dma_start(vblk(rank), T.v[:, :]).then_inc(sem.ld, 16)

    nv = [0]

    def chain():
        if nv[0]:
            ve.wait_ge(sem.vs, nv[0])

    def done(ins):
        ins.then_inc(sem.vs, 1)
        nv[0] += 1
        return nv[0]

    one_ready = done(ve.memset(T.one[0:C, 0:C], 1.0))
    chain(); done(ve.memset(T.neg[0:C, :], -0.5))

    left = 0
    for lsem, buf, name in ((sem.ldk, T.kd, "a%d" % rank), (sem.ldv, T.vd, "c%d" % rank)):
        g.wait_ge(lsem, 16)
        left += fused(hop1[rank], hop_masks(rank), buf[:, :], buf[:, :], sem[name], sem.h1)
    g.sync.wait_ge(sem.h1, left)
    g.sync.dma_start(T.qs[:, 0:C], T.q[:, 0:C]).then_inc(sem.ldq, 16)

    g.wait_ge(sem.ld, 32)
    sent = 0
    own = T.kv[:, rank * BW:(rank + 1) * BW]
    for d in direct[rank] + onchip[rank]:
        if hands_on(d, rank):
            sent += send(d, kblk(rank), kblk(rank), sem["a%d" % rank], sem.snd, mask_for(core, d))
            sent += send(d, vblk(rank), vblk(rank), sem["c%d" % rank], sem.snd, mask_for(core, d))
        else:
            sent += send(d, own, own, sem["a%d" % rank], sem.snd, mask_for(core, d))
    g.wait_ge(sem.vs, one_ready)
    g.affine_select(T.eye[0:C, 0:C], T.one[0:C, 0:C], [[-1, C]], AluOpType.is_equal, 0.0, 0, 1).then_inc(sem.idi, 1)
    for half, name, part in ((0, "a%d", kblk), (1, "c%d", vblk)):
        for (b, d) in relay[core]:
            g.wait_ge(sem[name % b], need[b][half])
            sent += send(d, part(b), part(b), sem[name % b], sem.snd, topo.mask(core, d))
    g.wait_ge(sem.snd, sent)

    sbank = [T.s0, T.s1, T.s2, T.s3, T.s4]
    tbank = [T.t0, T.t1]
    te.wait_ge(sem.ld, 32)
    te.wait_ge(sem.ldq, 16)
    red_done = []
    for i, j in enumerate(order[rank]):
        if j != rank:
            te.wait_ge(sem["a%d" % j], need[j][0])
        if i >= 2:
            te.wait_ge(sem.vs, red_done[i - 2])
        tb = tbank[i % 2]
        te.matmul(tb[0:C, 0:128], T.qs[:, 0:C], kblk(j), True, True).then_inc(sem["st%d" % i], 1)
        te.matmul(sbank[i][:, 0:C], kblk(j), T.qs[:, 0:C], True, False)
        chain()
        ve.wait_ge(sem["st%d" % i], 1)
        red_done.append(done(ve.tensor_reduce(T.mx[0:C, i:i + 1], tb[0:C, 0:128], AxisListType.X, AluOpType.max)))

    chain(); done(ve.tensor_reduce(T.mm[0:C, 0:1], T.mx[0:C, 0:NB], AxisListType.X, AluOpType.max))
    chain()
    ve.wait_ge(sem.idi, 1)
    d_ready = done(ve.tensor_scalar(T.dg[0:C, 0:C], T.eye[0:C, 0:C], T.mm[0:C, 0:1], None, AluOpType.mult))
    te.wait_ge(sem.vs, d_ready)
    for i in range(NB):
        te.matmul(sbank[i][:, 0:C], T.neg[0:C, 0:128], T.dg[0:C, 0:C], False, True).then_inc(sem["b%d" % i], 1)

    for i, j in enumerate(order[rank]):
        pj = T.p[:, i * 128:i * 128 + C]
        if i % 2 == 0:
            chain()
            ve.wait_ge(sem["b%d" % i], 1)
            te.wait_ge(sem.vs, done(ve.tensor_scalar(pj, sbank[i][:, 0:C], 0.0, None, AluOpType.max)))
        else:
            ac.wait_ge(sem["b%d" % i], 1)
            ac.activation(pj, sbank[i][:, 0:C], ActivationFunctionType.Relu).then_inc(sem["r%d" % i], 1)
            te.wait_ge(sem["r%d" % i], 1)
        if j != rank and need[j][1] is not None:
            te.wait_ge(sem["c%d" % j], need[j][1])
        ins = te.matmul(T.py[:, 0:C], vblk(j), pj, i == 0, i == NB - 1)
        if i == NB - 1:
            ins.then_inc(sem.yl, 1)
    chain()
    ve.wait_ge(sem.yl, 1)
    y_ready = done(ve.tensor_copy(T.yo[:, 0:C], T.py[:, 0:C]))

    g.sync.wait_ge(sem.vs, y_ready)
    g.sync.dma_start(T.y[:, 0:C], T.yo[:, 0:C]).then_inc(sem.sto, 16)
    g.sync.wait_ge(sem.sto, 16)
